import numpy as np
import ml_dtypes


def mxq(x, axis, fmt="e4m3"):
    dtype, down = {"e4m3": (ml_dtypes.float8_e4m3fn, 7), "e5m2": (ml_dtypes.float8_e5m2, 14)}[fmt]
    v = np.moveaxis(np.asarray(x, np.float32).astype(ml_dtypes.bfloat16).astype(np.float64), axis, -1)
    blocks = v.reshape(v.shape[:-1] + (-1, 32))
    amax = np.abs(blocks).max(-1, keepdims=True)
    byte = np.maximum(np.where(amax > 0, np.frexp(amax)[1] - 1 + 127, 0) - down, 1)
    scale = np.exp2(byte - 127.0)
    codes = (blocks / scale).astype(np.float32).astype(dtype).astype(np.float64)
    return np.moveaxis((codes * scale).reshape(v.shape), -1, axis)


WIDE = False


def mx_kscale(k):
    if not WIDE:
        return np.ones(k)
    levels = np.array([10, -10, 5, -5, 0])
    if k % 512:
        return np.exp2(np.random.permutation(np.resize(levels, k // 32))).repeat(32)
    a = np.empty((k // 512, 16))
    for p in range(k // 512):
        a[p, :8] = np.random.permutation(np.resize(levels, 8))
        for g in range(8):
            far = levels[np.abs(levels - a[p, g]) >= 10]
            a[p, g + 8] = far[np.random.randint(len(far))]
    return np.exp2(a.ravel()).repeat(32)


def f64(x):
    return np.asarray(x).astype(np.float64)


def striped(idx):
    return np.tile(idx.reshape(-1, 16).T, (8, 1)).astype(np.uint16)


def unstriped(offs):
    return offs[:16].T.reshape(-1).astype(np.int64)


E2M1 = np.array([0.0, 0.5, 1.0, 1.5, 2.0, 3.0, 4.0, 6.0, -0.0, -0.5, -1.0, -1.5, -2.0, -3.0, -4.0, -6.0])


def pack_weight(w, fmt):
    k, n = w.shape
    w = f64(np.asarray(w, np.float32).astype(ml_dtypes.bfloat16)).reshape(k // 32, 32, n)
    amax = np.abs(w).max(1)
    if fmt == "e4m3":
        byte = np.frexp(amax)[1] - 1 + 127 - 7
    else:
        mant, ex = np.frexp(amax / 6.0)
        byte = np.where(mant > 0.5, ex, ex - 1) + 127
    byte = np.clip(np.where(amax > 0, byte, 1), 1, 254)
    scaled = (w * np.exp2(127.0 - byte)[:, None, :]).reshape(k, n).astype(np.float32)
    by_word = np.ascontiguousarray(scaled.reshape(k // 512, 128, 4, n).transpose(0, 1, 3, 2))
    if fmt == "e4m3":
        words = by_word.astype(ml_dtypes.float8_e4m3fn).view(np.uint8)
    else:
        c = by_word.astype(ml_dtypes.float4_e2m1fn).view(np.uint8) & 0xF
        words = (c[..., 0::2] | (c[..., 1::2] << 4)).reshape(k // 512, 128, 2 * n)
    return np.ascontiguousarray(words), np.ascontiguousarray(byte.astype(np.uint8).reshape(k // 512, 16, n))


def unpack_weight(words, scales, fmt):
    g, _, n = scales.shape
    words = np.ascontiguousarray(words).reshape(g, 128, n, -1)
    if fmt == "e4m3":
        vals = words.view(ml_dtypes.float8_e4m3fn).astype(np.float64)
    else:
        nib = np.empty((g, 128, n, 4), np.uint8)
        nib[..., 0::2] = words & 0xF
        nib[..., 1::2] = words >> 4
        vals = E2M1[nib]
    vals = vals * np.repeat(np.exp2(scales.astype(np.float64) - 127.0), 8, axis=1)[..., None]
    return vals.transpose(0, 1, 3, 2).reshape(g * 512, n)


K, M, T, S = 512, 512, 2048, 1024


def setup_inputs():
    n = np.random.standard_normal
    s = mx_kscale(K)[:, None]
    u = mx_kscale(512)[:, None]
    v = pack_weight(n((K, T)) * s, "e4m3")
    p_w2 = pack_weight(1.4 * n((512, M)) / np.sqrt(512) / u, "e2m1")
    return {
        "tab_words": v[0],
        "tab_scales": v[1],
        "w1": (n((K, 512)) / np.sqrt(K) / s * u.T).astype(np.float32),
        "w2_words": p_w2[0],
        "w2_scales": p_w2[1],
        "ts": np.tile(np.exp(0.5 * n(T)), (128, 1)).astype(np.float32),
        "b": (0.3 * n(512)).astype(np.float32),
        "offs": striped(np.random.permutation(T)[:S]),
    }


def reference(tab_words, tab_scales, w1, w2_words, w2_scales, ts, b, offs):
    tab_ = unpack_weight(tab_words, tab_scales, "e4m3")[:, unstriped(offs)]
    w1_ = mxq(f64(w1), 0, "e4m3")
    w2_ = unpack_weight(w2_words, w2_scales, "e2m1")
    h_ = mxq(np.maximum(w1_.T @ tab_, 0.0), 0, "e4m3")
    y = w2_.T @ h_
    y = y * f64(ts)[0][unstriped(offs)]
    return y + f64(b)[:, None]

@@ -1,0 +1,170 @@
+from contextlib import ExitStack
+
+import concourse.mybir as mybir
+from concourse.masks import make_identity
+
+K, H, M, T, S = 512, 512, 512, 2048, 1024
+FLOPS = 2 * K * H * S + 2 * H * M * S
+P = 128
+F32, BF16 = mybir.dt.float32, mybir.dt.bfloat16
+I32, U32, U16, U8 = mybir.dt.int32, mybir.dt.uint32, mybir.dt.uint16, mybir.dt.uint8
+FP8X4, FP4X4 = mybir.dt.float8_e4m3fn_x4, mybir.dt.float4_e2m1fn_x4
+ACT = mybir.ActivationFunctionType
+MULT, ADD = mybir.AluOpType.mult, mybir.AluOpType.add
+CH = 256
+NCH = S // CH
+W1_ENG = ["S","V"]
+BIAS_ENG = ["G","G","G","S","S","S","S","S"]
+
+
+def tile_list_tabts_bias_kernel(tc, tab_words, tab_scales, w1, w2_words, w2_scales, ts, b, offs, out):
+    nc = tc.nc
+    with ExitStack() as ctx:
+        keep = ctx.enter_context(tc.tile_pool(name="keep", bufs=1))
+        hps = ctx.enter_context(tc.psum_pool(name="hps", bufs=4))
+        yps = ctx.enter_context(tc.psum_pool(name="yps", bufs=4))
+
+        offsets = keep.tile([P, S // 16], U16, name="offsets")
+        nc.sync.dma_start(offsets[:], offs)
+        ts_rows = keep.tile([P, 16], F32, name="ts_rows")
+        nc.sync.dma_start(ts_rows[:], ts[0].rearrange("(p c) -> p c", c=16))
+
+        tsc = keep.tile([P, T // 4], I32, name="tsc", align_bytes=64)
+        nc.gpsimd.memset(tsc[:], 0)
+        w2sc = keep.tile([P, M // 4], I32, name="w2sc", align_bytes=64)
+        ident = keep.tile([P, P], F32, name="ident")
+        make_identity(nc, ident[:])
+        nc.gpsimd.memset(w2sc[:], 0)
+        for q in range(4):
+            nc.sync.dma_start(tsc[32 * q : 32 * q + 4, :], tab_scales[0, 4 * q : 4 * q + 4, :].bitcast(I32))
+
+        nw = len(W1_ENG)
+        cw = H // nw
+        w1_raw = [keep.tile([P, 4, cw], F32, name="w1_raw%d" % h) for h in range(nw)]
+        words = keep.tile([P, T], I32, name="words", align_bytes=64)
+
+        def load_w1():
+            for h in range(nw):
+                nc.sync.dma_start(w1_raw[h][:], w1[:, h * cw : (h + 1) * cw].rearrange("(p j) c -> p j c", j=4))
+
+        def load_words():
+            nc.sync.dma_start(words[:], tab_words[0].rearrange("p t i -> p (t i)").bitcast(I32))
+
+        load_w1()
+        load_words()
+        w2w = keep.tile([P, 2 * M], U8, name="w2w", align_bytes=64)
+        nc.sync.dma_start(w2w[:].bitcast(I32), w2_words[0].bitcast(I32))
+        for q in range(4):
+            nc.sync.dma_start(w2sc[32 * q : 32 * q + 4, :], w2_scales[0, 4 * q : 4 * q + 4, :].bitcast(I32))
+        bias = keep.tile([P, 4], F32, name="bias")
+        with nc.allow_non_contiguous_dma(reason="one bias value a partition"):
+            nc.sync.dma_start(bias[:], b.rearrange("(c p) -> p c", p=P))
+
+        ts_all = keep.tile([P, T], F32, name="ts_all")
+        ts_view = ts_all[:].rearrange("m (p g c) -> m p g c", g=4, c=4)
+        for g in range(4):
+            bank = yps.tile([P, 4, P], F32, name="ybank")
+            for c in range(4):
+                nc.tensor.transpose(bank[:, c, :], ts_rows[:, 4 * g + c : 4 * g + c + 1].to_broadcast([P, P]), ident[:])
+            nc.scalar.copy(ts_view[:, :, g, :], bank[:].rearrange("m c p -> m p c"))
+
+        gsc = keep.tile([P, S], U8, name="gsc", align_bytes=64)
+        for h in range(2):
+            nc.vector.tensor_copy(gsc[:, 512 * h : 512 * (h + 1)], tsc[:].bitcast(U8).indirect(offsets[:, 32 * h : 32 * (h + 1)]))
+
+        w1_bf = keep.tile([P, 4, P, 4], BF16, name="w1_bf", align_bytes=64)
+        mw = cw // 4
+        for h in range(nw):
+            dst = w1_bf[:, :, h * mw : (h + 1) * mw, :].rearrange("p t m j -> p m t j")
+            src = w1_raw[h][:].rearrange("p j (m t) -> p m t j", t=4)
+            if W1_ENG[h] == "S":
+                nc.scalar.copy(dst, src)
+            elif W1_ENG[h] == "V":
+                nc.vector.tensor_copy(dst, src)
+            else:
+                nc.gpsimd.tensor_scalar(dst, src, 1.0, 0.0, MULT, ADD)
+        w1c = keep.tile([P, H], U32, name="w1c", align_bytes=64)
+        w1s = keep.tile([P, H], U8, name="w1s", align_bytes=64)
+        nc.vector.quantize_mx(w1c[:].bitcast(FP8X4), w1s[:], w1_bf[:].rearrange("p t m j -> p (t m j)"))
+
+        gw = [keep.tile([P, CH], U32, name="gw%d" % c, align_bytes=64) for c in range(NCH)]
+        gts = [keep.tile([P, CH], F32, name="gts%d" % c) for c in range(NCH)]
+        hb = [keep.tile([P, CH, 4], BF16, name="hb%d" % c, align_bytes=64) for c in range(NCH)]
+        hc = [keep.tile([P, CH], U32, name="hc%d" % c, align_bytes=64) for c in range(NCH)]
+        hs = [keep.tile([P, CH], U8, name="hs%d" % c, align_bytes=64) for c in range(NCH)]
+        ow = CH // 16
+
+        def gather_words(c):
+            nc.vector.tensor_copy(gw[c][:], words[:].bitcast(U32).indirect(offsets[:, ow * c : ow * (c + 1)]))
+
+        def gather_ts(c):
+            nc.vector.tensor_copy(gts[c][:], ts_all[:].indirect(offsets[:, ow * c : ow * (c + 1)]))
+
+        def layer1(c):
+            for u in range(CH // P):
+                bank = hps.tile([P, 4, P], F32, name="hbank")
+                for t in range(4):
+                    nc.tensor.matmul_mx(
+                        bank[:, t, :],
+                        lhsT=w1c[:, P * t : P * (t + 1)].bitcast(FP8X4),
+                        lhsT_scale=w1s[:, P * t : P * (t + 1)],
+                        rhs=gw[c][:, P * u : P * (u + 1)].bitcast(FP8X4),
+                        rhs_scale=gsc[:, CH * c + P * u : CH * c + P * (u + 1)],
+                        start=True,
+                        stop=True,
+                    )
+                nc.scalar.activation(hb[c][:, P * u : P * (u + 1), :], bank[:].rearrange("p t n -> p n t"), ACT.Relu)
+
+        def quant_h(c):
+            nc.vector.quantize_mx(hc[c][:].bitcast(FP8X4), hs[c][:], hb[c][:].rearrange("p n t -> p (n t)"))
+
+        def layer2(c):
+            for hp in range(2):
+                bank = yps.tile([P, 2, CH], F32, name="ybank")
+                for i in range(2):
+                    nt = 2 * hp + i
+                    nc.tensor.matmul_mx(
+                        bank[:, i, :],
+                        lhsT=w2w[:, 2 * P * nt : 2 * P * (nt + 1)].bitcast(FP4X4),
+                        lhsT_scale=w2sc[:].bitcast(U8)[:, P * nt : P * (nt + 1)],
+                        rhs=hc[c][:].bitcast(FP8X4),
+                        rhs_scale=hs[c][:],
+                        start=True,
+                        stop=True,
+                    )
+                prod = keep.tile([P, 2, CH], F32, name="prod%d_%d" % (c, hp))
+                nc.vector.tensor_tensor(prod[:], bank[:], gts[c][:].unsqueeze(1).to_broadcast([P, 2, CH]), MULT)
+                res = keep.tile([P, 2, CH], F32, name="res%d_%d" % (c, hp))
+                eng = BIAS_ENG[2 * c + hp]
+                for i in range(2):
+                    nt = 2 * hp + i
+                    if eng == "S":
+                        nc.scalar.activation(res[:, i, :], prod[:, i, :], ACT.Identity, bias=bias[:, nt : nt + 1])
+                    elif eng == "V":
+                        nc.vector.tensor_scalar(res[:, i, :], prod[:, i, :], bias[:, nt : nt + 1], None, ADD)
+                    else:
+                        nc.gpsimd.tensor_scalar(res[:, i, :], prod[:, i, :], 1.0, bias[:, nt : nt + 1], MULT, ADD)
+                nc.sync.dma_start(
+                    out[2 * P * hp : 2 * P * (hp + 1), CH * c : CH * (c + 1)].rearrange("(i p) j -> p i j", p=P), res[:]
+                )
+
+        gather_words(0)
+        layer1(0)
+        gather_words(1)
+        layer1(1)
+        quant_h(0)
+        gather_words(2)
+        layer1(2)
+        gather_words(3)
+        quant_h(1)
+        layer1(3)
+        quant_h(2)
+        quant_h(3)
+        gather_ts(0)
+        layer2(0)
+        gather_ts(1)
+        layer2(1)
+        gather_ts(2)
+        layer2(2)
+        gather_ts(3)
+        layer2(3)

@@ -13,8 +13,8 @@ ACT = mybir.ActivationFunctionType
 MULT, ADD = mybir.AluOpType.mult, mybir.AluOpType.add
 CH = 256
 NCH = S // CH
-W1_ENG = ["S","V"]
-BIAS_ENG = ["G","G","G","S","S","S","S","S"]
+W1_LOADS = [[0,320],[320,512]]
+W1_COPIES = [[0,0,320,"S"],[1,320,512,"V"]]
 
 
 def tile_list_tabts_bias_kernel(tc, tab_words, tab_scales, w1, w2_words, w2_scales, ts, b, offs, out):
@@ -24,28 +24,26 @@ def tile_list_tabts_bias_kernel(tc, tab_words, tab_scales, w1, w2_words, w2_scal
         hps = ctx.enter_context(tc.psum_pool(name="hps", bufs=4))
         yps = ctx.enter_context(tc.psum_pool(name="yps", bufs=4))
 
+        tsc = keep.tile([P, T // 4], I32, name="tsc", align_bytes=64)
+        nc.gpsimd.memset(tsc[:], 0)
+        ident = keep.tile([P, P], F32, name="ident")
+        make_identity(nc, ident[:])
+        w2sc = keep.tile([P, M // 4], I32, name="w2sc", align_bytes=64)
+        nc.gpsimd.memset(w2sc[:], 0)
+
         offsets = keep.tile([P, S // 16], U16, name="offsets")
         nc.sync.dma_start(offsets[:], offs)
         ts_rows = keep.tile([P, 16], F32, name="ts_rows")
         nc.sync.dma_start(ts_rows[:], ts[0].rearrange("(p c) -> p c", c=16))
-
-        tsc = keep.tile([P, T // 4], I32, name="tsc", align_bytes=64)
-        nc.gpsimd.memset(tsc[:], 0)
-        w2sc = keep.tile([P, M // 4], I32, name="w2sc", align_bytes=64)
-        ident = keep.tile([P, P], F32, name="ident")
-        make_identity(nc, ident[:])
-        nc.gpsimd.memset(w2sc[:], 0)
         for q in range(4):
             nc.sync.dma_start(tsc[32 * q : 32 * q + 4, :], tab_scales[0, 4 * q : 4 * q + 4, :].bitcast(I32))
 
-        nw = len(W1_ENG)
-        cw = H // nw
-        w1_raw = [keep.tile([P, 4, cw], F32, name="w1_raw%d" % h) for h in range(nw)]
+        w1_raw = [keep.tile([P, 4, c1 - c0], F32, name="w1_raw%d" % c0) for c0, c1 in W1_LOADS]
         words = keep.tile([P, T], I32, name="words", align_bytes=64)
 
         def load_w1():
-            for h in range(nw):
-                nc.sync.dma_start(w1_raw[h][:], w1[:, h * cw : (h + 1) * cw].rearrange("(p j) c -> p j c", j=4))
+            for h, (c0, c1) in enumerate(W1_LOADS):
+                nc.sync.dma_start(w1_raw[h][:], w1[:, c0:c1].rearrange("(p j) c -> p j c", j=4))
 
         def load_words():
             nc.sync.dma_start(words[:], tab_words[0].rearrange("p t i -> p (t i)").bitcast(I32))
@@ -69,102 +67,131 @@ def tile_list_tabts_bias_kernel(tc, tab_words, tab_scales, w1, w2_words, w2_scal
             nc.scalar.copy(ts_view[:, :, g, :], bank[:].rearrange("m c p -> m p c"))
 
         gsc = keep.tile([P, S], U8, name="gsc", align_bytes=64)
-        for h in range(2):
-            nc.vector.tensor_copy(gsc[:, 512 * h : 512 * (h + 1)], tsc[:].bitcast(U8).indirect(offsets[:, 32 * h : 32 * (h + 1)]))
-
+        gw = keep.tile([P, S], U32, name="gw", align_bytes=64)
+        gts_early = keep.tile([P, S // 2], F32, name="gts_early")
+        late = {}
         w1_bf = keep.tile([P, 4, P, 4], BF16, name="w1_bf", align_bytes=64)
-        mw = cw // 4
-        for h in range(nw):
-            dst = w1_bf[:, :, h * mw : (h + 1) * mw, :].rearrange("p t m j -> p m t j")
-            src = w1_raw[h][:].rearrange("p j (m t) -> p m t j", t=4)
-            if W1_ENG[h] == "S":
-                nc.scalar.copy(dst, src)
-            elif W1_ENG[h] == "V":
-                nc.vector.tensor_copy(dst, src)
-            else:
-                nc.gpsimd.tensor_scalar(dst, src, 1.0, 0.0, MULT, ADD)
         w1c = keep.tile([P, H], U32, name="w1c", align_bytes=64)
         w1s = keep.tile([P, H], U8, name="w1s", align_bytes=64)
-        nc.vector.quantize_mx(w1c[:].bitcast(FP8X4), w1s[:], w1_bf[:].rearrange("p t m j -> p (t m j)"))
+        hbs = [keep.tile([P, CH, 4], BF16, name="hb%d" % c, tag="hb%d" % c, align_bytes=64) for c in range(NCH)]
 
-        gw = [keep.tile([P, CH], U32, name="gw%d" % c, align_bytes=64) for c in range(NCH)]
-        gts = [keep.tile([P, CH], F32, name="gts%d" % c) for c in range(NCH)]
-        hb = [keep.tile([P, CH, 4], BF16, name="hb%d" % c, align_bytes=64) for c in range(NCH)]
-        hc = [keep.tile([P, CH], U32, name="hc%d" % c, align_bytes=64) for c in range(NCH)]
-        hs = [keep.tile([P, CH], U8, name="hs%d" % c, align_bytes=64) for c in range(NCH)]
-        ow = CH // 16
+        def hb(a, z):
+            c = a // CH
+            return hbs[c][:, a - c * CH : z - c * CH, :]
 
-        def gather_words(c):
-            nc.vector.tensor_copy(gw[c][:], words[:].bitcast(U32).indirect(offsets[:, ow * c : ow * (c + 1)]))
+        def gts(a, z):
+            return gts_early[:, a:z] if z <= S // 2 else late["gts"][:, a - S // 2 : z - S // 2]
 
-        def gather_ts(c):
-            nc.vector.tensor_copy(gts[c][:], ts_all[:].indirect(offsets[:, ow * c : ow * (c + 1)]))
+        def open_gts():
+            late["gts"] = keep.tile([P, S // 2], F32, name="gts_late", tag="hb0", align_bytes=64)
 
-        def layer1(c):
-            for u in range(CH // P):
+        hc = keep.tile([P, S], U32, name="hc", align_bytes=64)
+        hs = keep.tile([P, S], U8, name="hs", align_bytes=64)
+        prod = keep.tile([P, 4, S], F32, name="prod")
+        res = keep.tile([P, 4, S], F32, name="res")
+        out_v = out.rearrange("(i p) j -> p i j", p=P)
+
+        def prep_w1():
+            for h, c0, c1, eng in W1_COPIES:
+                base = W1_LOADS[h][0]
+                dst = w1_bf[:, :, c0 // 4 : c1 // 4, :].rearrange("p t m j -> p m j t")
+                src = w1_raw[h][:, :, c0 - base : c1 - base].rearrange("p j (m t) -> p m j t", t=4)
+                if eng == "S":
+                    nc.scalar.copy(dst, src)
+                elif eng == "V":
+                    nc.vector.tensor_copy(dst, src)
+                else:
+                    nc.gpsimd.tensor_scalar(dst, src, 1.0, 0.0, MULT, ADD)
+            nc.vector.quantize_mx(w1c[:].bitcast(FP8X4), w1s[:], w1_bf[:].rearrange("p t m j -> p (t m j)"))
+
+        def gather_scales(a, z):
+            nc.vector.tensor_copy(gsc[:, a:z], tsc[:].bitcast(U8).indirect(offsets[:, a // 16 : z // 16]))
+
+        def gather_words(a, z):
+            nc.vector.tensor_copy(gw[:, a:z], words[:].bitcast(U32).indirect(offsets[:, a // 16 : z // 16]))
+
+        def gather_ts(a, z):
+            nc.vector.tensor_copy(gts(a, z), ts_all[:].indirect(offsets[:, a // 16 : z // 16]))
+
+        def layer1(a, z, eng="S"):
+            for u in range(a, z, P):
                 bank = hps.tile([P, 4, P], F32, name="hbank")
                 for t in range(4):
                     nc.tensor.matmul_mx(
                         bank[:, t, :],
                         lhsT=w1c[:, P * t : P * (t + 1)].bitcast(FP8X4),
                         lhsT_scale=w1s[:, P * t : P * (t + 1)],
-                        rhs=gw[c][:, P * u : P * (u + 1)].bitcast(FP8X4),
-                        rhs_scale=gsc[:, CH * c + P * u : CH * c + P * (u + 1)],
+                        rhs=gw[:, u : u + P].bitcast(FP8X4),
+                        rhs_scale=gsc[:, u : u + P],
                         start=True,
                         stop=True,
                     )
-                nc.scalar.activation(hb[c][:, P * u : P * (u + 1), :], bank[:].rearrange("p t n -> p n t"), ACT.Relu)
+                if eng == "S":
+                    nc.scalar.activation(hb(u, u + P), bank[:].rearrange("p t n -> p n t"), ACT.Relu)
+                else:
+                    nc.vector.tensor_scalar(hb(u, u + P), bank[:].rearrange("p t n -> p n t"), 0.0, None, mybir.AluOpType.max)
 
-        def quant_h(c):
-            nc.vector.quantize_mx(hc[c][:].bitcast(FP8X4), hs[c][:], hb[c][:].rearrange("p n t -> p (n t)"))
+        def quant_h(a, z):
+            nc.vector.quantize_mx(hc[:, a:z].bitcast(FP8X4), hs[:, a:z], hb(a, z).rearrange("p n t -> p (n t)"))
 
-        def layer2(c):
-            for hp in range(2):
-                bank = yps.tile([P, 2, CH], F32, name="ybank")
-                for i in range(2):
-                    nt = 2 * hp + i
-                    nc.tensor.matmul_mx(
-                        bank[:, i, :],
-                        lhsT=w2w[:, 2 * P * nt : 2 * P * (nt + 1)].bitcast(FP4X4),
-                        lhsT_scale=w2sc[:].bitcast(U8)[:, P * nt : P * (nt + 1)],
-                        rhs=hc[c][:].bitcast(FP8X4),
-                        rhs_scale=hs[c][:],
-                        start=True,
-                        stop=True,
-                    )
-                prod = keep.tile([P, 2, CH], F32, name="prod%d_%d" % (c, hp))
-                nc.vector.tensor_tensor(prod[:], bank[:], gts[c][:].unsqueeze(1).to_broadcast([P, 2, CH]), MULT)
-                res = keep.tile([P, 2, CH], F32, name="res%d_%d" % (c, hp))
-                eng = BIAS_ENG[2 * c + hp]
-                for i in range(2):
-                    nt = 2 * hp + i
-                    if eng == "S":
-                        nc.scalar.activation(res[:, i, :], prod[:, i, :], ACT.Identity, bias=bias[:, nt : nt + 1])
-                    elif eng == "V":
-                        nc.vector.tensor_scalar(res[:, i, :], prod[:, i, :], bias[:, nt : nt + 1], None, ADD)
-                    else:
-                        nc.gpsimd.tensor_scalar(res[:, i, :], prod[:, i, :], 1.0, bias[:, nt : nt + 1], MULT, ADD)
-                nc.sync.dma_start(
-                    out[2 * P * hp : 2 * P * (hp + 1), CH * c : CH * (c + 1)].rearrange("(i p) j -> p i j", p=P), res[:]
+        def layer2(a, z, n0, n1):
+            w = z - a
+            bank = yps.tile([P, n1 - n0, w], F32, name="ybank")
+            for nt in range(n0, n1):
+                nc.tensor.matmul_mx(
+                    bank[:, nt - n0, :],
+                    lhsT=w2w[:, 2 * P * nt : 2 * P * (nt + 1)].bitcast(FP4X4),
+                    lhsT_scale=w2sc[:].bitcast(U8)[:, P * nt : P * (nt + 1)],
+                    rhs=hc[:, a:z].bitcast(FP8X4),
+                    rhs_scale=hs[:, a:z],
+                    start=True,
+                    stop=True,
                 )
+            nc.vector.tensor_tensor(prod[:, n0:n1, a:z], bank[:], gts(a, z).unsqueeze(1).to_broadcast([P, n1 - n0, w]), MULT)
 
-        gather_words(0)
-        layer1(0)
-        gather_words(1)
-        layer1(1)
-        quant_h(0)
-        gather_words(2)
-        layer1(2)
-        gather_words(3)
-        quant_h(1)
-        layer1(3)
-        quant_h(2)
-        quant_h(3)
-        gather_ts(0)
-        layer2(0)
-        gather_ts(1)
-        layer2(1)
-        gather_ts(2)
-        layer2(2)
-        gather_ts(3)
-        layer2(3)
+        def finish(a, z, n0, n1, eng):
+            for nt in range(n0, n1):
+                if eng == "S":
+                    nc.scalar.activation(res[:, nt, a:z], prod[:, nt, a:z], ACT.Identity, bias=bias[:, nt : nt + 1])
+                elif eng == "V":
+                    nc.vector.tensor_scalar(res[:, nt, a:z], prod[:, nt, a:z], bias[:, nt : nt + 1], None, ADD)
+                else:
+                    nc.gpsimd.tensor_scalar(res[:, nt, a:z], prod[:, nt, a:z], 1.0, bias[:, nt : nt + 1], MULT, ADD)
+            nc.sync.dma_start(out_v[:, n0:n1, a:z], res[:, n0:n1, a:z])
+
+        gather_scales(0, 1024)
+        prep_w1()
+        gather_words(0, 256)
+        layer1(0, 256)
+        gather_words(256, 512)
+        layer1(256, 512)
+        quant_h(0, 256)
+        open_gts()
+        gather_words(512, 1024)
+        quant_h(256, 512)
+        gather_ts(0, 256)
+        layer2(0, 256, 0, 2)
+        layer2(0, 256, 2, 4)
+        layer1(512, 768)
+        finish(0, 256, 0, 2, "G")
+        finish(0, 256, 2, 4, "S")
+        quant_h(512, 768)
+        gather_ts(256, 512)
+        layer2(256, 512, 0, 2)
+        layer2(256, 512, 2, 4)
+        layer1(768, 1024)
+        finish(256, 512, 0, 2, "G")
+        finish(256, 512, 2, 4, "S")
+        quant_h(768, 1024)
+        gather_ts(512, 768)
+        layer2(512, 768, 0, 2)
+        finish(512, 768, 0, 2, "S")
+        layer2(512, 768, 2, 4)
+        finish(512, 768, 2, 4, "S")
+        gather_ts(768, 1024)
+        layer2(768, 1024, 0, 2)
+        finish(768, 1024, 0, 2, "S")
+        layer2(768, 1024, 2, 3)
+        layer2(768, 1024, 3, 4)
+        finish(768, 1024, 2, 3, "S")
+        finish(768, 1024, 3, 4, "V")

@@ -173,24 +173,31 @@ def tile_list_tabts_bias_kernel(tc, tab_words, tab_scales, w1, w2_words, w2_scal
         layer2(0, 256, 0, 2)
         layer2(0, 256, 2, 4)
         layer1(512, 768)
-        finish(0, 256, 0, 2, "G")
-        finish(0, 256, 2, 4, "S")
+        finish(0, 256, 0, 1, "G")
+        finish(0, 256, 1, 2, "G")
+        finish(0, 256, 2, 3, "S")
+        finish(0, 256, 3, 4, "S")
         quant_h(512, 768)
         gather_ts(256, 512)
         layer2(256, 512, 0, 2)
         layer2(256, 512, 2, 4)
         layer1(768, 1024)
-        finish(256, 512, 0, 2, "G")
-        finish(256, 512, 2, 4, "S")
+        finish(256, 512, 0, 1, "G")
+        finish(256, 512, 1, 2, "G")
+        finish(256, 512, 2, 3, "S")
+        finish(256, 512, 3, 4, "S")
         quant_h(768, 1024)
         gather_ts(512, 768)
         layer2(512, 768, 0, 2)
-        finish(512, 768, 0, 2, "S")
+        finish(512, 768, 0, 1, "S")
+        finish(512, 768, 1, 2, "S")
         layer2(512, 768, 2, 4)
-        finish(512, 768, 2, 4, "S")
+        finish(512, 768, 2, 3, "S")
+        finish(512, 768, 3, 4, "S")
         gather_ts(768, 1024)
         layer2(768, 1024, 0, 2)
-        finish(768, 1024, 0, 2, "S")
+        finish(768, 1024, 0, 1, "S")
+        finish(768, 1024, 1, 2, "S")
         layer2(768, 1024, 2, 3)
         layer2(768, 1024, 3, 4)
         finish(768, 1024, 2, 3, "S")

@@ -11,135 +11,112 @@ I32, U32, U16, U8 = mybir.dt.int32, mybir.dt.uint32, mybir.dt.uint16, mybir.dt.u
 FP8X4, FP4X4 = mybir.dt.float8_e4m3fn_x4, mybir.dt.float4_e2m1fn_x4
 ACT = mybir.ActivationFunctionType
 MULT, ADD = mybir.AluOpType.mult, mybir.AluOpType.add
-CH = 256
-NCH = S // CH
-W1_LOADS = [[0,320],[320,512]]
-W1_COPIES = [[0,0,320,"S"],[1,320,512,"V"]]
+W1_LOADS = [(0, 320), (320, 512)]
+CHUNKS = [(0, 128), (128, 256), (256, 512), (512, 768), (768, 896), (896, 1024)]
+WORD_PARTS = [(0, 128), (128, 512), (512, 1024)]
 
 
 def tile_list_tabts_bias_kernel(tc, tab_words, tab_scales, w1, w2_words, w2_scales, ts, b, offs, out):
     nc = tc.nc
     with ExitStack() as ctx:
         keep = ctx.enter_context(tc.tile_pool(name="keep", bufs=1))
-        hps = ctx.enter_context(tc.psum_pool(name="hps", bufs=4))
-        yps = ctx.enter_context(tc.psum_pool(name="yps", bufs=4))
+        psum = ctx.enter_context(tc.psum_pool(name="psum", bufs=1))
 
-        tsc = keep.tile([P, T // 4], I32, name="tsc", align_bytes=64)
+        def bank(i, shape):
+            return psum.tile(shape, F32, name="bank%d" % i, tag="bank%d" % i)
+
+        tsc = keep.tile([P, T // 4], I32, name="tsc", tag="slot_sc", align_bytes=64)
         nc.gpsimd.memset(tsc[:], 0)
         ident = keep.tile([P, P], F32, name="ident")
         make_identity(nc, ident[:])
-        w2sc = keep.tile([P, M // 4], I32, name="w2sc", align_bytes=64)
-        nc.gpsimd.memset(w2sc[:], 0)
+        gsc = keep.tile([P, S // 4], I32, name="gsc", align_bytes=64)
+        nc.gpsimd.memset(gsc[:], 0)
 
+        ts_rows = keep.tile([P, 16], F32, name="ts_rows", tag="slot_w1", align_bytes=64)
+        nc.sync.dma_start(ts_rows[:], ts[0].rearrange("(p c) -> p c", c=16))
         offsets = keep.tile([P, S // 16], U16, name="offsets")
         nc.sync.dma_start(offsets[:], offs)
-        ts_rows = keep.tile([P, 16], F32, name="ts_rows")
-        nc.sync.dma_start(ts_rows[:], ts[0].rearrange("(p c) -> p c", c=16))
-        for q in range(4):
-            nc.sync.dma_start(tsc[32 * q : 32 * q + 4, :], tab_scales[0, 4 * q : 4 * q + 4, :].bitcast(I32))
+        nc.sync.dma_start(tsc[0:16, :], tab_scales[0].bitcast(I32))
 
-        w1_raw = [keep.tile([P, 4, c1 - c0], F32, name="w1_raw%d" % c0) for c0, c1 in W1_LOADS]
+        w1_raw = [keep.tile([P, 4, c1 - c0], F32, name="w1_raw%d" % c0, tag="w1_raw%d" % c0, align_bytes=64) for c0, c1 in W1_LOADS]
         words = keep.tile([P, T], I32, name="words", align_bytes=64)
-
-        def load_w1():
-            for h, (c0, c1) in enumerate(W1_LOADS):
-                nc.sync.dma_start(w1_raw[h][:], w1[:, c0:c1].rearrange("(p j) c -> p j c", j=4))
-
-        def load_words():
-            nc.sync.dma_start(words[:], tab_words[0].rearrange("p t i -> p (t i)").bitcast(I32))
-
-        load_w1()
-        load_words()
+        for h, (c0, c1) in enumerate(W1_LOADS):
+            nc.sync.dma_start(w1_raw[h][:], w1[:, c0:c1].rearrange("(p j) c -> p j c", j=4))
+        nc.sync.dma_start(words[:], tab_words[0].rearrange("p t i -> p (t i)").bitcast(I32))
         w2w = keep.tile([P, 2 * M], U8, name="w2w", align_bytes=64)
         nc.sync.dma_start(w2w[:].bitcast(I32), w2_words[0].bitcast(I32))
-        for q in range(4):
-            nc.sync.dma_start(w2sc[32 * q : 32 * q + 4, :], w2_scales[0, 4 * q : 4 * q + 4, :].bitcast(I32))
-        bias = keep.tile([P, 4], F32, name="bias")
-        with nc.allow_non_contiguous_dma(reason="one bias value a partition"):
-            nc.sync.dma_start(bias[:], b.rearrange("(c p) -> p c", p=P))
 
-        ts_all = keep.tile([P, T], F32, name="ts_all")
+        ts_all = keep.tile([P, T], F32, name="ts_all", tag="slot_ts", align_bytes=64)
         ts_view = ts_all[:].rearrange("m (p g c) -> m p g c", g=4, c=4)
         for g in range(4):
-            bank = yps.tile([P, 4, P], F32, name="ybank")
+            tb = bank(g, [P, 4, P])
             for c in range(4):
-                nc.tensor.transpose(bank[:, c, :], ts_rows[:, 4 * g + c : 4 * g + c + 1].to_broadcast([P, P]), ident[:])
-            nc.scalar.copy(ts_view[:, :, g, :], bank[:].rearrange("m c p -> m p c"))
+                nc.tensor.transpose(tb[:, c, :], ts_rows[:, 4 * g + c : 4 * g + c + 1].to_broadcast([P, P]), ident[:])
+            nc.scalar.copy(ts_view[:, :, g, :], tb[:].rearrange("m c p -> m p c"))
 
-        gsc = keep.tile([P, S], U8, name="gsc", align_bytes=64)
-        gw = keep.tile([P, S], U32, name="gw", align_bytes=64)
-        gts_early = keep.tile([P, S // 2], F32, name="gts_early")
-        late = {}
-        w1_bf = keep.tile([P, 4, P, 4], BF16, name="w1_bf", align_bytes=64)
+        gsc16 = keep.tile([P, S], U8, name="gsc16", align_bytes=64)
+        gts = {}
         w1c = keep.tile([P, H], U32, name="w1c", align_bytes=64)
         w1s = keep.tile([P, H], U8, name="w1s", align_bytes=64)
-        hbs = [keep.tile([P, CH, 4], BF16, name="hb%d" % c, tag="hb%d" % c, align_bytes=64) for c in range(NCH)]
-
-        def hb(a, z):
-            c = a // CH
-            return hbs[c][:, a - c * CH : z - c * CH, :]
-
-        def gts(a, z):
-            return gts_early[:, a:z] if z <= S // 2 else late["gts"][:, a - S // 2 : z - S // 2]
-
-        def open_gts():
-            late["gts"] = keep.tile([P, S // 2], F32, name="gts_late", tag="hb0", align_bytes=64)
-
         hc = keep.tile([P, S], U32, name="hc", align_bytes=64)
         hs = keep.tile([P, S], U8, name="hs", align_bytes=64)
         prod = keep.tile([P, 4, S], F32, name="prod")
         res = keep.tile([P, 4, S], F32, name="res")
         out_v = out.rearrange("(i p) j -> p i j", p=P)
+        gw = {}
+        hb = {}
 
         def prep_w1():
-            for h, c0, c1, eng in W1_COPIES:
-                base = W1_LOADS[h][0]
+            w1_bf = keep.tile([P, 4, P, 4], BF16, name="w1_bf", tag="slot_w1", align_bytes=64)
+            for h, (c0, c1) in enumerate(W1_LOADS):
                 dst = w1_bf[:, :, c0 // 4 : c1 // 4, :].rearrange("p t m j -> p m j t")
-                src = w1_raw[h][:, :, c0 - base : c1 - base].rearrange("p j (m t) -> p m j t", t=4)
-                if eng == "S":
-                    nc.scalar.copy(dst, src)
-                elif eng == "V":
+                src = w1_raw[h][:].rearrange("p j (m t) -> p m j t", t=4)
+                if h == 0:
                     nc.vector.tensor_copy(dst, src)
                 else:
-                    nc.gpsimd.tensor_scalar(dst, src, 1.0, 0.0, MULT, ADD)
+                    nc.scalar.copy(dst, src)
+            return w1_bf
+
+        def quant_w1(w1_bf):
             nc.vector.quantize_mx(w1c[:].bitcast(FP8X4), w1s[:], w1_bf[:].rearrange("p t m j -> p (t m j)"))
 
-        def gather_scales(a, z):
-            nc.vector.tensor_copy(gsc[:, a:z], tsc[:].bitcast(U8).indirect(offsets[:, a // 16 : z // 16]))
-
         def gather_words(a, z):
-            nc.vector.tensor_copy(gw[:, a:z], words[:].bitcast(U32).indirect(offsets[:, a // 16 : z // 16]))
+            nc.vector.tensor_copy(gw[0][:, a:z], words[:].bitcast(U32).indirect(offsets[:, a // 16 : z // 16]))
 
-        def gather_ts(a, z):
-            nc.vector.tensor_copy(gts(a, z), ts_all[:].indirect(offsets[:, a // 16 : z // 16]))
-
-        def layer1(a, z, eng="S"):
+        def gather_ts(a, z, slot):
+            g = keep.tile([P, z - a], F32, name="gts%d" % a, tag=slot, align_bytes=64)
+            nc.vector.tensor_copy(g[:], ts_all[:].indirect(offsets[:, a // 16 : z // 16]))
             for u in range(a, z, P):
-                bank = hps.tile([P, 4, P], F32, name="hbank")
+                gts[u] = (g, a)
+
+        def layer1(c, banks):
+            a, z = CHUNKS[c]
+            hb[c] = keep.tile([P, z - a, 4], BF16, name="hb%d" % c, tag="hb%d" % c, align_bytes=64)
+            for u, bi in zip(range(a, z, P), banks):
+                hbank = bank(bi, [P, 4, P])
                 for t in range(4):
                     nc.tensor.matmul_mx(
-                        bank[:, t, :],
+                        hbank[:, t, :],
                         lhsT=w1c[:, P * t : P * (t + 1)].bitcast(FP8X4),
                         lhsT_scale=w1s[:, P * t : P * (t + 1)],
-                        rhs=gw[:, u : u + P].bitcast(FP8X4),
-                        rhs_scale=gsc[:, u : u + P],
+                        rhs=gw[0][:, u : u + P].bitcast(FP8X4),
+                        rhs_scale=gsc[:].bitcast(U8)[:, u : u + P],
                         start=True,
                         stop=True,
                     )
-                if eng == "S":
-                    nc.scalar.activation(hb(u, u + P), bank[:].rearrange("p t n -> p n t"), ACT.Relu)
-                else:
-                    nc.vector.tensor_scalar(hb(u, u + P), bank[:].rearrange("p t n -> p n t"), 0.0, None, mybir.AluOpType.max)
+                nc.scalar.activation(hb[c][:, u - a : u - a + P, :], hbank[:].rearrange("p t n -> p n t"), ACT.Relu)
 
-        def quant_h(a, z):
-            nc.vector.quantize_mx(hc[:, a:z].bitcast(FP8X4), hs[:, a:z], hb(a, z).rearrange("p n t -> p (n t)"))
+        def quant_h(c):
+            a, z = CHUNKS[c]
+            nc.vector.quantize_mx(hc[:, a:z].bitcast(FP8X4), hs[:, a:z], hb[c][:].rearrange("p n t -> p (n t)"))
 
-        def layer2(a, z, n0, n1):
+        def layer2(c, n0, n1, bi):
+            a, z = CHUNKS[c]
             w = z - a
-            bank = yps.tile([P, n1 - n0, w], F32, name="ybank")
+            ybank = bank(bi, [P, n1 - n0, w])
             for nt in range(n0, n1):
                 nc.tensor.matmul_mx(
-                    bank[:, nt - n0, :],
+                    ybank[:, nt - n0, :],
                     lhsT=w2w[:, 2 * P * nt : 2 * P * (nt + 1)].bitcast(FP4X4),
                     lhsT_scale=w2sc[:].bitcast(U8)[:, P * nt : P * (nt + 1)],
                     rhs=hc[:, a:z].bitcast(FP8X4),
@@ -147,58 +124,63 @@ def tile_list_tabts_bias_kernel(tc, tab_words, tab_scales, w1, w2_words, w2_scal
                     start=True,
                     stop=True,
                 )
-            nc.vector.tensor_tensor(prod[:, n0:n1, a:z], bank[:], gts(a, z).unsqueeze(1).to_broadcast([P, n1 - n0, w]), MULT)
+            nc.vector.tensor_tensor(prod[:, n0:n1, a:z], ybank[:], gts[a][0][:, a - gts[a][1] : z - gts[a][1]].unsqueeze(1).to_broadcast([P, n1 - n0, w]), MULT)
 
-        def finish(a, z, n0, n1, eng):
-            for nt in range(n0, n1):
-                if eng == "S":
-                    nc.scalar.activation(res[:, nt, a:z], prod[:, nt, a:z], ACT.Identity, bias=bias[:, nt : nt + 1])
-                elif eng == "V":
-                    nc.vector.tensor_scalar(res[:, nt, a:z], prod[:, nt, a:z], bias[:, nt : nt + 1], None, ADD)
-                else:
-                    nc.gpsimd.tensor_scalar(res[:, nt, a:z], prod[:, nt, a:z], 1.0, bias[:, nt : nt + 1], MULT, ADD)
-            nc.sync.dma_start(out_v[:, n0:n1, a:z], res[:, n0:n1, a:z])
+        def finish(a, z, nt, eng, store=1):
+            if eng == "S":
+                nc.scalar.activation(res[:, nt, a:z], prod[:, nt, a:z], ACT.Identity, bias=bias[:, nt : nt + 1])
+            elif eng == "V":
+                nc.vector.tensor_scalar(res[:, nt, a:z], prod[:, nt, a:z], bias[:, nt : nt + 1], None, ADD)
+            else:
+                nc.gpsimd.tensor_scalar(res[:, nt, a:z], prod[:, nt, a:z], 1.0, bias[:, nt : nt + 1], MULT, ADD)
+            if store:
+                nc.sync.dma_start(out_v[:, nt + 1 - store : nt + 1, a:z], res[:, nt + 1 - store : nt + 1, a:z])
 
-        gather_scales(0, 1024)
-        prep_w1()
+        nc.vector.tensor_copy(gsc16[:], tsc[:].bitcast(U8).indirect(offsets[:]))
+        for q in range(4):
+            nc.sync.dma_start(gsc[32 * q : 32 * q + 4, :], gsc16[4 * q : 4 * q + 4, :].bitcast(I32))
+        w2sc = keep.tile([P, M // 4], I32, name="w2sc", tag="slot_sc", align_bytes=64)
+        nc.gpsimd.memset(w2sc[:], 0)
+        for q in range(4):
+            nc.sync.dma_start(w2sc[32 * q : 32 * q + 4, :], w2_scales[0, 4 * q : 4 * q + 4, :].bitcast(I32))
+        w1_bf = prep_w1()
+        bias = keep.tile([P, 4], F32, name="bias", tag="w1_raw0", align_bytes=64)
+        with nc.allow_non_contiguous_dma(reason="one bias value a partition"):
+            nc.sync.dma_start(bias[:], b.rearrange("(c p) -> p c", p=P))
+        gather_ts(0, 256, "gts0")
+        quant_w1(w1_bf)
+        gw[0] = keep.tile([P, S], U32, name="gw", tag="w1_raw320", align_bytes=64)
         gather_words(0, 256)
-        layer1(0, 256)
-        gather_words(256, 512)
-        layer1(256, 512)
-        quant_h(0, 256)
-        open_gts()
-        gather_words(512, 1024)
-        quant_h(256, 512)
-        gather_ts(0, 256)
-        layer2(0, 256, 0, 2)
-        layer2(0, 256, 2, 4)
-        layer1(512, 768)
-        finish(0, 256, 0, 1, "G")
-        finish(0, 256, 1, 2, "G")
-        finish(0, 256, 2, 3, "S")
-        finish(0, 256, 3, 4, "S")
-        quant_h(512, 768)
-        gather_ts(256, 512)
-        layer2(256, 512, 0, 2)
-        layer2(256, 512, 2, 4)
-        layer1(768, 1024)
-        finish(256, 512, 0, 1, "G")
-        finish(256, 512, 1, 2, "G")
-        finish(256, 512, 2, 3, "S")
-        finish(256, 512, 3, 4, "S")
-        quant_h(768, 1024)
-        gather_ts(512, 768)
-        layer2(512, 768, 0, 2)
-        finish(512, 768, 0, 1, "S")
-        finish(512, 768, 1, 2, "S")
-        layer2(512, 768, 2, 4)
-        finish(512, 768, 2, 3, "S")
-        finish(512, 768, 3, 4, "S")
-        gather_ts(768, 1024)
-        layer2(768, 1024, 0, 2)
-        finish(768, 1024, 0, 1, "S")
-        finish(768, 1024, 1, 2, "S")
-        layer2(768, 1024, 2, 3)
-        layer2(768, 1024, 3, 4)
-        finish(768, 1024, 2, 3, "S")
-        finish(768, 1024, 3, 4, "V")
+        layer1(0, [4])
+        layer1(1, [5])
+        gather_words(256, 1024)
+        layer1(2, [6, 7])
+        gather_ts(256, 512, "slot_w1")
+        quant_h(0)
+        gather_ts(512, 1024, "hb0")
+        quant_h(1)
+        layer2(0, 0, 4, 5)
+        layer1(3, [0, 1])
+        quant_h(2)
+        layer2(1, 0, 4, 7)
+        layer1(4, [2])
+        layer1(5, [3])
+        quant_h(3)
+        layer2(2, 0, 2, 1)
+        layer2(2, 2, 4, 4)
+        for nt in range(4):
+            finish(0, 256, nt, "G")
+            finish(256, 512, nt, "S")
+        quant_h(4)
+        layer2(3, 0, 2, 2)
+        quant_h(5)
+        layer2(3, 2, 4, 3)
+        for nt in range(4):
+            finish(512, 768, nt, "GGSS"[nt])
+        layer2(4, 0, 4, 6)
+        for nt in range(4):
+            finish(768, 896, nt, "S", 4 * (nt == 3))
+        layer2(5, 0, 2, 0)
+        layer2(5, 2, 4, 5)
+        for nt in range(4):
+            finish(896, 1024, nt, "SSVV"[nt], 4 * (nt == 3))

@@ -12,7 +12,7 @@ FP8X4, FP4X4 = mybir.dt.float8_e4m3fn_x4, mybir.dt.float4_e2m1fn_x4
 ACT = mybir.ActivationFunctionType
 MULT, ADD = mybir.AluOpType.mult, mybir.AluOpType.add
 W1_LOADS = [(0, 320), (320, 512)]
-CHUNKS = [(0, 128), (128, 256), (256, 512), (512, 768), (768, 896), (896, 1024)]
+CHUNKS = [(0, 128), (128, 256), (256, 512), (512, 768), (768, 1024)]
 WORD_PARTS = [(0, 128), (128, 512), (512, 1024)]
 
 
@@ -54,7 +54,7 @@ def tile_list_tabts_bias_kernel(tc, tab_words, tab_scales, w1, w2_words, w2_scal
                 nc.tensor.transpose(tb[:, c, :], ts_rows[:, 4 * g + c : 4 * g + c + 1].to_broadcast([P, P]), ident[:])
             nc.scalar.copy(ts_view[:, :, g, :], tb[:].rearrange("m c p -> m p c"))
 
-        gsc16 = keep.tile([P, S], U8, name="gsc16", align_bytes=64)
+        gsc16 = keep.tile([P, S], U8, name="gsc16", tag="gsc16", align_bytes=64)
         gts = {}
         w1c = keep.tile([P, H], U32, name="w1c", align_bytes=64)
         w1s = keep.tile([P, H], U8, name="w1s", align_bytes=64)
@@ -144,7 +144,7 @@ def tile_list_tabts_bias_kernel(tc, tab_words, tab_scales, w1, w2_words, w2_scal
         for q in range(4):
             nc.sync.dma_start(w2sc[32 * q : 32 * q + 4, :], w2_scales[0, 4 * q : 4 * q + 4, :].bitcast(I32))
         w1_bf = prep_w1()
-        bias = keep.tile([P, 4], F32, name="bias", tag="w1_raw0", align_bytes=64)
+        bias = keep.tile([P, 4], F32, name="bias", tag="gsc16", align_bytes=64)
         with nc.allow_non_contiguous_dma(reason="one bias value a partition"):
             nc.sync.dma_start(bias[:], b.rearrange("(c p) -> p c", p=P))
         gather_ts(0, 256, "gts0")
@@ -163,24 +163,21 @@ def tile_list_tabts_bias_kernel(tc, tab_words, tab_scales, w1, w2_words, w2_scal
         layer1(3, [0, 1])
         quant_h(2)
         layer2(1, 0, 4, 7)
-        layer1(4, [2])
-        layer1(5, [3])
+        layer1(4, [2, 3])
         quant_h(3)
+        for nt in range(4):
+            finish(0, 256, nt, "GSSG"[nt])
         layer2(2, 0, 2, 1)
         layer2(2, 2, 4, 4)
         for nt in range(4):
-            finish(0, 256, nt, "G")
-            finish(256, 512, nt, "S")
+            finish(256, 512, nt, "SG"[nt % 2])
         quant_h(4)
-        layer2(3, 0, 2, 2)
-        quant_h(5)
-        layer2(3, 2, 4, 3)
+        layer2(3, 0, 2, 3)
+        layer2(3, 2, 4, 6)
         for nt in range(4):
-            finish(512, 768, nt, "GGSS"[nt])
-        layer2(4, 0, 4, 6)
+            finish(512, 768, nt, "SGSS"[nt])
+        layer2(4, 0, 2, 0)
+        layer2(4, 2, 3, 2)
+        layer2(4, 3, 4, 5)
         for nt in range(4):
-            finish(768, 896, nt, "S", 4 * (nt == 3))
-        layer2(5, 0, 2, 0)
-        layer2(5, 2, 4, 5)
-        for nt in range(4):
-            finish(896, 1024, nt, "SSVV"[nt], 4 * (nt == 3))
+            finish(768, 1024, nt, "SGSV"[nt])

@@ -26,7 +26,8 @@ def tile_list_tabts_bias_kernel(tc, tab_words, tab_scales, w1, w2_words, w2_scal
             return psum.tile(shape, F32, name="bank%d" % i, tag="bank%d" % i)
 
         tsc = keep.tile([P, T // 4], I32, name="tsc", tag="slot_sc", align_bytes=64)
-        nc.gpsimd.memset(tsc[:], 0)
+        nc.gpsimd.memset(tsc[:, 0 : T // 8], 0)
+        nc.vector.memset(tsc[:, T // 8 : T // 4], 0)
         ident = keep.tile([P, P], F32, name="ident")
         make_identity(nc, ident[:])
         gsc = keep.tile([P, S // 4], I32, name="gsc", align_bytes=64)
@@ -38,10 +39,9 @@ def tile_list_tabts_bias_kernel(tc, tab_words, tab_scales, w1, w2_words, w2_scal
         nc.sync.dma_start(offsets[:], offs)
         nc.sync.dma_start(tsc[0:16, :], tab_scales[0].bitcast(I32))
 
-        w1_raw = [keep.tile([P, 4, c1 - c0], F32, name="w1_raw%d" % c0, tag="w1_raw%d" % c0, align_bytes=64) for c0, c1 in W1_LOADS]
+        w1_raw = keep.tile([P, 4, H], F32, name="w1_raw", tag="w1_raw", align_bytes=64)
         words = keep.tile([P, T], I32, name="words", align_bytes=64)
-        for h, (c0, c1) in enumerate(W1_LOADS):
-            nc.sync.dma_start(w1_raw[h][:], w1[:, c0:c1].rearrange("(p j) c -> p j c", j=4))
+        nc.sync.dma_start(w1_raw[:], w1.rearrange("(p j) c -> p j c", j=4))
         nc.sync.dma_start(words[:], tab_words[0].rearrange("p t i -> p (t i)").bitcast(I32))
         w2w = keep.tile([P, 2 * M], U8, name="w2w", align_bytes=64)
         nc.sync.dma_start(w2w[:].bitcast(I32), w2_words[0].bitcast(I32))
@@ -70,7 +70,7 @@ def tile_list_tabts_bias_kernel(tc, tab_words, tab_scales, w1, w2_words, w2_scal
             w1_bf = keep.tile([P, 4, P, 4], BF16, name="w1_bf", tag="slot_w1", align_bytes=64)
             for h, (c0, c1) in enumerate(W1_LOADS):
                 dst = w1_bf[:, :, c0 // 4 : c1 // 4, :].rearrange("p t m j -> p m j t")
-                src = w1_raw[h][:].rearrange("p j (m t) -> p m j t", t=4)
+                src = w1_raw[:, :, c0:c1].rearrange("p j (m t) -> p m j t", t=4)
                 if h == 0:
                     nc.vector.tensor_copy(dst, src)
                 else:
@@ -111,7 +111,7 @@ def tile_list_tabts_bias_kernel(tc, tab_words, tab_scales, w1, w2_words, w2_scal
             nc.vector.quantize_mx(hc[:, a:z].bitcast(FP8X4), hs[:, a:z], hb[c][:].rearrange("p n t -> p (n t)"))
 
         def layer2(c, n0, n1, bi):
-            a, z = CHUNKS[c]
+            a, z = (0, 256) if c == 0 else CHUNKS[c]
             w = z - a
             ybank = bank(bi, [P, n1 - n0, w])
             for nt in range(n0, n1):
@@ -149,35 +149,40 @@ def tile_list_tabts_bias_kernel(tc, tab_words, tab_scales, w1, w2_words, w2_scal
             nc.sync.dma_start(bias[:], b.rearrange("(c p) -> p c", p=P))
         gather_ts(0, 256, "gts0")
         quant_w1(w1_bf)
-        gw[0] = keep.tile([P, S], U32, name="gw", tag="w1_raw320", align_bytes=64)
+        gw[0] = keep.tile([P, S], U32, name="gw", tag="w1_raw", align_bytes=64)
         gather_words(0, 256)
         layer1(0, [4])
         layer1(1, [5])
-        gather_words(256, 1024)
+        gather_words(256, 512)
         layer1(2, [6, 7])
+        gather_words(512, 1024)
         gather_ts(256, 512, "slot_w1")
         quant_h(0)
-        gather_ts(512, 1024, "hb0")
         quant_h(1)
-        layer2(0, 0, 4, 5)
+        gather_ts(512, 1024, "hb1")
         layer1(3, [0, 1])
+        layer2(0, 0, 1, 6)
+        finish(0, 256, 0, "G")
         quant_h(2)
-        layer2(1, 0, 4, 7)
+        layer2(0, 1, 2, 7)
+        finish(0, 256, 1, "G")
+        layer2(0, 2, 4, 0)
         layer1(4, [2, 3])
         quant_h(3)
-        for nt in range(4):
-            finish(0, 256, nt, "GSSG"[nt])
+        finish(0, 256, 2, "S")
+        finish(0, 256, 3, "G")
         layer2(2, 0, 2, 1)
-        layer2(2, 2, 4, 4)
+        layer2(2, 2, 4, 2)
         for nt in range(4):
             finish(256, 512, nt, "SG"[nt % 2])
         quant_h(4)
         layer2(3, 0, 2, 3)
-        layer2(3, 2, 4, 6)
+        layer2(3, 2, 4, 5)
         for nt in range(4):
-            finish(512, 768, nt, "SGSS"[nt])
-        layer2(4, 0, 2, 0)
-        layer2(4, 2, 3, 2)
-        layer2(4, 3, 4, 5)
+            finish(512, 768, nt, "SGSG"[nt])
+        layer2(4, 0, 1, 0)
+        layer2(4, 1, 2, 7)
+        layer2(4, 2, 3, 4)
+        layer2(4, 3, 4, 6)
         for nt in range(4):
-            finish(768, 1024, nt, "SGSV"[nt])
+            finish(768, 1024, nt, "SSVV"[nt])

@@ -161,28 +161,28 @@ def tile_list_tabts_bias_kernel(tc, tab_words, tab_scales, w1, w2_words, w2_scal
         quant_h(1)
         gather_ts(512, 1024, "hb1")
         layer1(3, [0, 1])
-        layer2(0, 0, 1, 6)
+        layer2(0, 0, 1, 5)
         finish(0, 256, 0, "G")
         quant_h(2)
         layer2(0, 1, 2, 7)
-        finish(0, 256, 1, "G")
+        finish(0, 256, 1, "S")
         layer2(0, 2, 4, 0)
-        layer1(4, [2, 3])
+        layer1(4, [6, 2])
         quant_h(3)
-        finish(0, 256, 2, "S")
-        finish(0, 256, 3, "G")
+        finish(0, 256, 2, "G")
+        finish(0, 256, 3, "S")
         layer2(2, 0, 2, 1)
-        layer2(2, 2, 4, 2)
+        layer2(2, 2, 4, 6)
         for nt in range(4):
             finish(256, 512, nt, "SG"[nt % 2])
         quant_h(4)
-        layer2(3, 0, 2, 3)
+        layer2(3, 0, 2, 2)
         layer2(3, 2, 4, 5)
         for nt in range(4):
             finish(512, 768, nt, "SGSG"[nt])
         layer2(4, 0, 1, 0)
         layer2(4, 1, 2, 7)
         layer2(4, 2, 3, 4)
-        layer2(4, 3, 4, 6)
+        layer2(4, 3, 4, 3)
         for nt in range(4):
             finish(768, 1024, nt, "SSVV"[nt])

@@ -11,7 +11,7 @@ I32, U32, U16, U8 = mybir.dt.int32, mybir.dt.uint32, mybir.dt.uint16, mybir.dt.u
 FP8X4, FP4X4 = mybir.dt.float8_e4m3fn_x4, mybir.dt.float4_e2m1fn_x4
 ACT = mybir.ActivationFunctionType
 MULT, ADD = mybir.AluOpType.mult, mybir.AluOpType.add
-W1_LOADS = [(0, 320), (320, 512)]
+W1_LOADS = [(0, 352), (352, 512)]
 CHUNKS = [(0, 128), (128, 256), (256, 512), (512, 768), (768, 1024)]
 WORD_PARTS = [(0, 128), (128, 512), (512, 1024)]
 
@@ -26,25 +26,23 @@ def tile_list_tabts_bias_kernel(tc, tab_words, tab_scales, w1, w2_words, w2_scal
             return psum.tile(shape, F32, name="bank%d" % i, tag="bank%d" % i)
 
         tsc = keep.tile([P, T // 4], I32, name="tsc", tag="slot_sc", align_bytes=64)
-        nc.gpsimd.memset(tsc[:, 0 : T // 8], 0)
-        nc.vector.memset(tsc[:, T // 8 : T // 4], 0)
+        nc.gpsimd.memset(tsc[32:64, :], 0)
+        nc.vector.memset(tsc[64:P, :], 0)
         ident = keep.tile([P, P], F32, name="ident")
         make_identity(nc, ident[:])
         gsc = keep.tile([P, S // 4], I32, name="gsc", align_bytes=64)
         nc.gpsimd.memset(gsc[:], 0)
 
         ts_rows = keep.tile([P, 16], F32, name="ts_rows", tag="slot_w1", align_bytes=64)
-        nc.sync.dma_start(ts_rows[:], ts[0].rearrange("(p c) -> p c", c=16))
+        nc.scalar.dma_start(ts_rows[:], ts[0].rearrange("(p c) -> p c", c=16))
         offsets = keep.tile([P, S // 16], U16, name="offsets")
         nc.sync.dma_start(offsets[:], offs)
-        nc.sync.dma_start(tsc[0:16, :], tab_scales[0].bitcast(I32))
+        nc.sync.dma_start(tsc[0:32, :], tab_scales[0].bitcast(I32).unsqueeze(1).to_broadcast([16, 2, T // 4]))
 
         w1_raw = keep.tile([P, 4, H], F32, name="w1_raw", tag="w1_raw", align_bytes=64)
         words = keep.tile([P, T], I32, name="words", align_bytes=64)
         nc.sync.dma_start(w1_raw[:], w1.rearrange("(p j) c -> p j c", j=4))
         nc.sync.dma_start(words[:], tab_words[0].rearrange("p t i -> p (t i)").bitcast(I32))
-        w2w = keep.tile([P, 2 * M], U8, name="w2w", align_bytes=64)
-        nc.sync.dma_start(w2w[:].bitcast(I32), w2_words[0].bitcast(I32))
 
         ts_all = keep.tile([P, T], F32, name="ts_all", tag="slot_ts", align_bytes=64)
         ts_view = ts_all[:].rearrange("m (p g c) -> m p g c", g=4, c=4)
@@ -118,7 +116,7 @@ def tile_list_tabts_bias_kernel(tc, tab_words, tab_scales, w1, w2_words, w2_scal
                 nc.tensor.matmul_mx(
                     ybank[:, nt - n0, :],
                     lhsT=w2w[:, 2 * P * nt : 2 * P * (nt + 1)].bitcast(FP4X4),
-                    lhsT_scale=w2sc[:].bitcast(U8)[:, P * nt : P * (nt + 1)],
+                    lhsT_scale=w2sc.bitcast(U8)[:, P * nt : P * (nt + 1)],
                     rhs=hc[:, a:z].bitcast(FP8X4),
                     rhs_scale=hs[:, a:z],
                     start=True,
@@ -138,9 +136,12 @@ def tile_list_tabts_bias_kernel(tc, tab_words, tab_scales, w1, w2_words, w2_scal
 
         nc.vector.tensor_copy(gsc16[:], tsc[:].bitcast(U8).indirect(offsets[:]))
         for q in range(4):
-            nc.sync.dma_start(gsc[32 * q : 32 * q + 4, :], gsc16[4 * q : 4 * q + 4, :].bitcast(I32))
-        w2sc = keep.tile([P, M // 4], I32, name="w2sc", tag="slot_sc", align_bytes=64)
-        nc.gpsimd.memset(w2sc[:], 0)
+            nc.sync.dma_start(gsc[32 * q : 32 * q + 4, :], gsc16[8 * q : 8 * q + 8 : 2, :].bitcast(I32))
+        w2_bytes = keep.tile([P, M // 2 + M // 4], I32, name="w2_bytes", tag="slot_sc", align_bytes=64)
+        w2w = w2_bytes[:, 0 : M // 2].bitcast(U8)
+        w2sc = w2_bytes[:, M // 2 : M // 2 + M // 4]
+        nc.sync.dma_start(w2_bytes[:, 0 : M // 2], w2_words[0].bitcast(I32))
+        nc.gpsimd.memset(w2sc, 0)
         for q in range(4):
             nc.sync.dma_start(w2sc[32 * q : 32 * q + 4, :], w2_scales[0, 4 * q : 4 * q + 4, :].bitcast(I32))
         w1_bf = prep_w1()

@@ -176,11 +176,12 @@ def tile_list_tabts_bias_kernel(tc, tab_words, tab_scales, w1, w2_words, w2_scal
         layer2(2, 2, 4, 6)
         for nt in range(4):
             finish(256, 512, nt, "SG"[nt % 2])
+        layer2(3, 0, 2, 5)
         quant_h(4)
-        layer2(3, 0, 2, 2)
-        layer2(3, 2, 4, 5)
+        layer2(3, 2, 3, 2)
+        layer2(3, 3, 4, 1)
         for nt in range(4):
-            finish(512, 768, nt, "SGSG"[nt])
+            finish(512, 768, nt, "SGSS"[nt])
         layer2(4, 0, 1, 0)
         layer2(4, 1, 2, 7)
         layer2(4, 2, 3, 4)

@@ -122,7 +122,8 @@ def tile_list_tabts_bias_kernel(tc, tab_words, tab_scales, w1, w2_words, w2_scal
                     start=True,
                     stop=True,
                 )
-            nc.vector.tensor_tensor(prod[:, n0:n1, a:z], ybank[:], gts[a][0][:, a - gts[a][1] : z - gts[a][1]].unsqueeze(1).to_broadcast([P, n1 - n0, w]), MULT)
+            for nt in range(n0, n1):
+                nc.vector.tensor_tensor(prod[:, nt, a:z], ybank[:, nt - n0, :], gts[a][0][:, a - gts[a][1] : z - gts[a][1]], MULT)
 
         def finish(a, z, nt, eng, store=1):
             if eng == "S":
@@ -170,8 +171,8 @@ def tile_list_tabts_bias_kernel(tc, tab_words, tab_scales, w1, w2_words, w2_scal
         layer2(0, 2, 4, 0)
         layer1(4, [6, 2])
         quant_h(3)
-        finish(0, 256, 2, "G")
-        finish(0, 256, 3, "S")
+        finish(0, 256, 2, "S")
+        finish(0, 256, 3, "G")
         layer2(2, 0, 2, 1)
         layer2(2, 2, 4, 6)
         for nt in range(4):

from contextlib import ExitStack

import concourse.mybir as mybir
from concourse.masks import make_identity

K, H, M, T, S = 512, 512, 512, 2048, 1024
FLOPS = 2 * K * H * S + 2 * H * M * S
P = 128
F32, BF16 = mybir.dt.float32, mybir.dt.bfloat16
I32, U32, U16, U8 = mybir.dt.int32, mybir.dt.uint32, mybir.dt.uint16, mybir.dt.uint8
FP8X4, FP4X4 = mybir.dt.float8_e4m3fn_x4, mybir.dt.float4_e2m1fn_x4
ACT = mybir.ActivationFunctionType
MULT, ADD = mybir.AluOpType.mult, mybir.AluOpType.add
W1_LOADS = [(0, 352), (352, 512)]
CHUNKS = [(0, 128), (128, 256), (256, 512), (512, 768), (768, 1024)]
WORD_PARTS = [(0, 128), (128, 512), (512, 1024)]


def tile_list_tabts_bias_kernel(tc, tab_words, tab_scales, w1, w2_words, w2_scales, ts, b, offs, out):
    nc = tc.nc
    with ExitStack() as ctx:
        keep = ctx.enter_context(tc.tile_pool(name="keep", bufs=1))
        psum = ctx.enter_context(tc.psum_pool(name="psum", bufs=1))

        def bank(i, shape):
            return psum.tile(shape, F32, name="bank%d" % i, tag="bank%d" % i)

        tsc = keep.tile([P, T // 4], I32, name="tsc", tag="slot_sc", align_bytes=64)
        nc.gpsimd.memset(tsc[32:64, :], 0)
        nc.vector.memset(tsc[64:P, :], 0)
        ident = keep.tile([P, P], F32, name="ident")
        make_identity(nc, ident[:])
        gsc = keep.tile([P, S // 4], I32, name="gsc", align_bytes=64)
        nc.gpsimd.memset(gsc[:], 0)

        ts_rows = keep.tile([P, 16], F32, name="ts_rows", tag="slot_w1", align_bytes=64)
        nc.scalar.dma_start(ts_rows[:], ts[0].rearrange("(p c) -> p c", c=16))
        offsets = keep.tile([P, S // 16], U16, name="offsets")
        nc.sync.dma_start(offsets[:], offs)
        nc.sync.dma_start(tsc[0:32, :], tab_scales[0].bitcast(I32).unsqueeze(1).to_broadcast([16, 2, T // 4]))

        w1_raw = keep.tile([P, 4, H], F32, name="w1_raw", tag="w1_raw", align_bytes=64)
        words = keep.tile([P, T], I32, name="words", align_bytes=64)
        nc.sync.dma_start(w1_raw[:], w1.rearrange("(p j) c -> p j c", j=4))
        nc.sync.dma_start(words[:], tab_words[0].rearrange("p t i -> p (t i)").bitcast(I32))

        ts_all = keep.tile([P, T], F32, name="ts_all", tag="slot_ts", align_bytes=64)
        ts_view = ts_all[:].rearrange("m (p g c) -> m p g c", g=4, c=4)
        for g in range(4):
            tb = bank(g, [P, 4, P])
            for c in range(4):
                nc.tensor.transpose(tb[:, c, :], ts_rows[:, 4 * g + c : 4 * g + c + 1].to_broadcast([P, P]), ident[:])
            nc.scalar.copy(ts_view[:, :, g, :], tb[:].rearrange("m c p -> m p c"))

        gsc16 = keep.tile([P, S], U8, name="gsc16", tag="gsc16", align_bytes=64)
        gts = {}
        w1c = keep.tile([P, H], U32, name="w1c", align_bytes=64)
        w1s = keep.tile([P, H], U8, name="w1s", align_bytes=64)
        hc = keep.tile([P, S], U32, name="hc", align_bytes=64)
        hs = keep.tile([P, S], U8, name="hs", align_bytes=64)
        prod = keep.tile([P, 4, S], F32, name="prod")
        res = keep.tile([P, 4, S], F32, name="res")
        out_v = out.rearrange("(i p) j -> p i j", p=P)
        gw = {}
        hb = {}

        def prep_w1():
            w1_bf = keep.tile([P, 4, P, 4], BF16, name="w1_bf", tag="slot_w1", align_bytes=64)
            for h, (c0, c1) in enumerate(W1_LOADS):
                dst = w1_bf[:, :, c0 // 4 : c1 // 4, :].rearrange("p t m j -> p m j t")
                src = w1_raw[:, :, c0:c1].rearrange("p j (m t) -> p m j t", t=4)
                if h == 0:
                    nc.vector.tensor_copy(dst, src)
                else:
                    nc.scalar.copy(dst, src)
            return w1_bf

        def quant_w1(w1_bf):
            nc.vector.quantize_mx(w1c[:].bitcast(FP8X4), w1s[:], w1_bf[:].rearrange("p t m j -> p (t m j)"))

        def gather_words(a, z):
            nc.vector.tensor_copy(gw[0][:, a:z], words[:].bitcast(U32).indirect(offsets[:, a // 16 : z // 16]))

        def gather_ts(a, z, slot):
            g = keep.tile([P, z - a], F32, name="gts%d" % a, tag=slot, align_bytes=64)
            nc.vector.tensor_copy(g[:], ts_all[:].indirect(offsets[:, a // 16 : z // 16]))
            for u in range(a, z, P):
                gts[u] = (g, a)

        def layer1(c, banks):
            a, z = CHUNKS[c]
            hb[c] = keep.tile([P, z - a, 4], BF16, name="hb%d" % c, tag="hb%d" % c, align_bytes=64)
            for u, bi in zip(range(a, z, P), banks):
                hbank = bank(bi, [P, 4, P])
                for t in range(4):
                    nc.tensor.matmul_mx(
                        hbank[:, t, :],
                        lhsT=w1c[:, P * t : P * (t + 1)].bitcast(FP8X4),
                        lhsT_scale=w1s[:, P * t : P * (t + 1)],
                        rhs=gw[0][:, u : u + P].bitcast(FP8X4),
                        rhs_scale=gsc[:].bitcast(U8)[:, u : u + P],
                        start=True,
                        stop=True,
                    )
                nc.scalar.activation(hb[c][:, u - a : u - a + P, :], hbank[:].rearrange("p t n -> p n t"), ACT.Relu)

        def quant_h(c):
            a, z = CHUNKS[c]
            nc.vector.quantize_mx(hc[:, a:z].bitcast(FP8X4), hs[:, a:z], hb[c][:].rearrange("p n t -> p (n t)"))

        def layer2(c, n0, n1, bi):
            a, z = (0, 256) if c == 0 else CHUNKS[c]
            w = z - a
            ybank = bank(bi, [P, n1 - n0, w])
            for nt in range(n0, n1):
                nc.tensor.matmul_mx(
                    ybank[:, nt - n0, :],
                    lhsT=w2w[:, 2 * P * nt : 2 * P * (nt + 1)].bitcast(FP4X4),
                    lhsT_scale=w2sc.bitcast(U8)[:, P * nt : P * (nt + 1)],
                    rhs=hc[:, a:z].bitcast(FP8X4),
                    rhs_scale=hs[:, a:z],
                    start=True,
                    stop=True,
                )
            for nt in range(n0, n1):
                nc.vector.tensor_tensor(prod[:, nt, a:z], ybank[:, nt - n0, :], gts[a][0][:, a - gts[a][1] : z - gts[a][1]], MULT)

        def finish(a, z, nt, eng, store=1):
            if eng == "S":
                nc.scalar.activation(res[:, nt, a:z], prod[:, nt, a:z], ACT.Identity, bias=bias[:, nt : nt + 1])
            elif eng == "V":
                nc.vector.tensor_scalar(res[:, nt, a:z], prod[:, nt, a:z], bias[:, nt : nt + 1], None, ADD)
            else:
                nc.gpsimd.tensor_scalar(res[:, nt, a:z], prod[:, nt, a:z], 1.0, bias[:, nt : nt + 1], MULT, ADD)
            if store:
                nc.sync.dma_start(out_v[:, nt + 1 - store : nt + 1, a:z], res[:, nt + 1 - store : nt + 1, a:z])

        nc.vector.tensor_copy(gsc16[:], tsc[:].bitcast(U8).indirect(offsets[:]))
        for q in range(4):
            nc.sync.dma_start(gsc[32 * q : 32 * q + 4, :], gsc16[8 * q : 8 * q + 8 : 2, :].bitcast(I32))
        w2_bytes = keep.tile([P, M // 2 + M // 4], I32, name="w2_bytes", tag="slot_sc", align_bytes=64)
        w2w = w2_bytes[:, 0 : M // 2].bitcast(U8)
        w2sc = w2_bytes[:, M // 2 : M // 2 + M // 4]
        nc.sync.dma_start(w2_bytes[:, 0 : M // 2], w2_words[0].bitcast(I32))
        nc.gpsimd.memset(w2sc, 0)
        for q in range(4):
            nc.sync.dma_start(w2sc[32 * q : 32 * q + 4, :], w2_scales[0, 4 * q : 4 * q + 4, :].bitcast(I32))
        w1_bf = prep_w1()
        bias = keep.tile([P, 4], F32, name="bias", tag="gsc16", align_bytes=64)
        with nc.allow_non_contiguous_dma(reason="one bias value a partition"):
            nc.sync.dma_start(bias[:], b.rearrange("(c p) -> p c", p=P))
        gather_ts(0, 256, "gts0")
        quant_w1(w1_bf)
        gw[0] = keep.tile([P, S], U32, name="gw", tag="w1_raw", align_bytes=64)
        gather_words(0, 256)
        layer1(0, [4])
        layer1(1, [5])
        gather_words(256, 512)
        layer1(2, [6, 7])
        gather_words(512, 1024)
        gather_ts(256, 512, "slot_w1")
        quant_h(0)
        quant_h(1)
        gather_ts(512, 1024, "hb1")
        layer1(3, [0, 1])
        layer2(0, 0, 1, 5)
        finish(0, 256, 0, "G")
        quant_h(2)
        layer2(0, 1, 2, 7)
        finish(0, 256, 1, "S")
        layer2(0, 2, 4, 0)
        layer1(4, [6, 2])
        quant_h(3)
        finish(0, 256, 2, "S")
        finish(0, 256, 3, "G")
        layer2(2, 0, 2, 1)
        layer2(2, 2, 4, 6)
        for nt in range(4):
            finish(256, 512, nt, "SG"[nt % 2])
        layer2(3, 0, 2, 5)
        quant_h(4)
        layer2(3, 2, 3, 2)
        layer2(3, 3, 4, 1)
        for nt in range(4):
            finish(512, 768, nt, "SGSS"[nt])
        layer2(4, 0, 1, 0)
        layer2(4, 1, 2, 7)
        layer2(4, 2, 3, 4)
        layer2(4, 3, 4, 3)
        for nt in range(4):
            finish(768, 1024, nt, "SSVV"[nt])
